import numpy as np
import ml_dtypes


def mxq(x, axis, fmt="e4m3"):
    dtype, down = {"e4m3": (ml_dtypes.float8_e4m3fn, 7), "e5m2": (ml_dtypes.float8_e5m2, 14)}[fmt]
    v = np.moveaxis(np.asarray(x, np.float32).astype(ml_dtypes.bfloat16).astype(np.float64), axis, -1)
    blocks = v.reshape(v.shape[:-1] + (-1, 32))
    amax = np.abs(blocks).max(-1, keepdims=True)
    byte = np.maximum(np.where(amax > 0, np.frexp(amax)[1] - 1 + 127, 0) - down, 1)
    scale = np.exp2(byte - 127.0)
    codes = (blocks / scale).astype(np.float32).astype(dtype).astype(np.float64)
    return np.moveaxis((codes * scale).reshape(v.shape), -1, axis)


WIDE = False


def mx_kscale(k):
    if not WIDE:
        return np.ones(k)
    levels = np.array([10, -10, 5, -5, 0])
    if k % 512:
        return np.exp2(np.random.permutation(np.resize(levels, k // 32))).repeat(32)
    a = np.empty((k // 512, 16))
    for p in range(k // 512):
        a[p, :8] = np.random.permutation(np.resize(levels, 8))
        for g in range(8):
            far = levels[np.abs(levels - a[p, g]) >= 10]
            a[p, g + 8] = far[np.random.randint(len(far))]
    return np.exp2(a.ravel()).repeat(32)


def f64(x):
    return np.asarray(x).astype(np.float64)


E2M1 = np.array([0.0, 0.5, 1.0, 1.5, 2.0, 3.0, 4.0, 6.0, -0.0, -0.5, -1.0, -1.5, -2.0, -3.0, -4.0, -6.0])


def pack_weight(w, fmt):
    k, n = w.shape
    w = f64(np.asarray(w, np.float32).astype(ml_dtypes.bfloat16)).reshape(k // 32, 32, n)
    amax = np.abs(w).max(1)
    if fmt == "e4m3":
        byte = np.frexp(amax)[1] - 1 + 127 - 7
    else:
        mant, ex = np.frexp(amax / 6.0)
        byte = np.where(mant > 0.5, ex, ex - 1) + 127
    byte = np.clip(np.where(amax > 0, byte, 1), 1, 254)
    scaled = (w * np.exp2(127.0 - byte)[:, None, :]).reshape(k, n).astype(np.float32)
    by_word = np.ascontiguousarray(scaled.reshape(k // 512, 128, 4, n).transpose(0, 1, 3, 2))
    if fmt == "e4m3":
        words = by_word.astype(ml_dtypes.float8_e4m3fn).view(np.uint8)
    else:
        c = by_word.astype(ml_dtypes.float4_e2m1fn).view(np.uint8) & 0xF
        words = (c[..., 0::2] | (c[..., 1::2] << 4)).reshape(k // 512, 128, 2 * n)
    return np.ascontiguousarray(words), np.ascontiguousarray(byte.astype(np.uint8).reshape(k // 512, 16, n))


def unpack_weight(words, scales, fmt):
    g, _, n = scales.shape
    words = np.ascontiguousarray(words).reshape(g, 128, n, -1)
    if fmt == "e4m3":
        vals = words.view(ml_dtypes.float8_e4m3fn).astype(np.float64)
    else:
        nib = np.empty((g, 128, n, 4), np.uint8)
        nib[..., 0::2] = words & 0xF
        nib[..., 1::2] = words >> 4
        vals = E2M1[nib]
    vals = vals * np.repeat(np.exp2(scales.astype(np.float64) - 127.0), 8, axis=1)[..., None]
    return vals.transpose(0, 1, 3, 2).reshape(g * 512, n)


K, L, T, R, N = 1024, 512, 512, 512, 512


def setup_inputs():
    n = np.random.standard_normal
    fk = mx_kscale(K)
    fr = mx_kscale(R)
    fl = mx_kscale(L)
    xtp = pack_weight(n((K, T)) / fk[:, None], "e4m3")
    wap = pack_weight(n((K, R)) * 1 / np.sqrt(K) * fk[:, None] * fr, "e2m1")
    xqp = pack_weight(n((L, T)) / fl[:, None], "e4m3")
    wcp = pack_weight(n((L, R)) * 1 / np.sqrt(L) * fl[:, None] * fr, "e2m1")
    wbp = pack_weight(n((R, N)) * 1 / np.sqrt(R) / fr[:, None], "e4m3")
    wyp = pack_weight(n((K, N)) * 1 / np.sqrt(K) * fk[:, None], "e2m1")
    return {
        "xt_words": xtp[0],
        "xt_scales": xtp[1],
        "wa_words": wap[0],
        "wa_scales": wap[1],
        "xq_words": xqp[0],
        "xq_scales": xqp[1],
        "wc_words": wcp[0],
        "wc_scales": wcp[1],
        "wb_words": wbp[0],
        "wb_scales": wbp[1],
        "wy_words": wyp[0],
        "wy_scales": wyp[1],
    }


def reference(xt_words, xt_scales, wa_words, wa_scales, xq_words, xq_scales, wc_words, wc_scales, wb_words, wb_scales, wy_words, wy_scales):
    xtu = unpack_weight(xt_words, xt_scales, "e4m3")
    wau = unpack_weight(wa_words, wa_scales, "e2m1")
    xqu = unpack_weight(xq_words, xq_scales, "e4m3")
    wcu = unpack_weight(wc_words, wc_scales, "e2m1")
    wbu = unpack_weight(wb_words, wb_scales, "e4m3")
    wyu = unpack_weight(wy_words, wy_scales, "e2m1")
    z = wau.T @ xtu + wcu.T @ xqu
    zp = np.pad(z, ((0, 0), (1, 0)))[:, :T]
    hid = np.maximum(z, zp)
    hidq = mxq(hid, 0, "e4m3")
    y = wbu.T @ hidq + wyu.T @ xtu
    return y

@@ -1,0 +1,181 @@
+from contextlib import ExitStack
+
+import concourse.mybir as mybir
+from concourse.masks import make_identity
+
+K, L, T, R, N = 1024, 512, 512, 512, 512
+FLOPS = 2 * T * (K * R + L * R + R * N + K * N)
+
+F32 = mybir.dt.float32
+BF16 = mybir.dt.bfloat16
+I32 = mybir.dt.int32
+U32 = mybir.dt.uint32
+U8 = mybir.dt.uint8
+FP8X4 = mybir.dt.float8_e4m3fn_x4
+FP4X4 = mybir.dt.float4_e2m1fn_x4
+
+P = 128
+CHUNKS = T // P
+PAD = 32
+
+
+def tile_mix_hidden_peak_with_before_kernel(
+    tc, xt_words, xt_scales, wa_words, wa_scales, xq_words, xq_scales,
+    wc_words, wc_scales, wb_words, wb_scales, wy_words, wy_scales, out,
+):
+    nc = tc.nc
+    with ExitStack() as ctx:
+        sb = ctx.enter_context(tc.tile_pool(name="sb", bufs=1))
+        ps = ctx.enter_context(tc.psum_pool(name="ps", bufs=1))
+        ctx.enter_context(tc.manual_schedule())
+
+        def plane(engine, name, scales):
+            t = sb.tile([P, scales.shape[0], 512], U8, name=name, align_bytes=64)
+            engine.memset(t[:].bitcast(I32), 0)
+            return t
+
+        def load_scale_rows(queue, t, scales, r):
+            rows = scales.rearrange("z (q r) c -> r q z c", r=4)
+            queue.dma_start(out=t[r:P:32, :, :].bitcast(I32), in_=rows[r].bitcast(I32))
+
+        def load_fp8(queue, name, words):
+            t = sb.tile([P, 512], U32, name=name, align_bytes=64)
+            queue.dma_start(out=t[:].bitcast(I32), in_=words.rearrange("p n b -> p (n b)").bitcast(I32))
+            return t
+
+        def load_fp4(queue, name, words):
+            t = sb.tile([P, words.shape[0], 1024], U8, name=name, align_bytes=64)
+            queue.dma_start(out=t[:].bitcast(I32), in_=words.rearrange("z p b -> p z b").bitcast(I32))
+            return t
+
+        xt_s = plane(nc.vector, "xt_s", xt_scales)
+        wa_s = plane(nc.gpsimd, "wa_s", wa_scales)
+        xq_s = plane(nc.vector, "xq_s", xq_scales)
+        wy_s = plane(nc.vector, "wy_s", wy_scales)
+        wc_s = plane(nc.vector, "wc_s", wc_scales)
+        wb_s = plane(nc.vector, "wb_s", wb_scales)
+        zb = sb.tile([P, PAD + 4 * T], BF16, name="zb", align_bytes=64)
+        nc.vector.memset(zb[:, 0:PAD], 0.0)
+
+        wa_w = [load_fp4(nc.scalar, "wa_w0", wa_words[0:1])]
+        xt_w = [load_fp8(nc.scalar, "xt_w0", xt_words[0])]
+        load_scale_rows(nc.gpsimd, wa_s, wa_scales, 3)
+        for r in range(4):
+            load_scale_rows(nc.sync, xt_s, xt_scales, r)
+        for r in range(3):
+            load_scale_rows(nc.sync, wa_s, wa_scales, r)
+        for r in range(4):
+            load_scale_rows(nc.gpsimd, wy_s, wy_scales, r)
+        xt_w.append(load_fp8(nc.sync, "xt_w1", xt_words[1]))
+        wa_w.append(load_fp4(nc.sync, "wa_w1", wa_words[1:2]))
+        for r in range(4):
+            load_scale_rows(nc.sync, xq_s, xq_scales, r)
+        xq_w = load_fp8(nc.sync, "xq_w", xq_words[0])
+        wc_w = load_fp4(nc.sync, "wc_w", wc_words)
+        for r in range(4):
+            load_scale_rows(nc.sync, wc_s, wc_scales, r)
+        wy_w = load_fp4(nc.sync, "wy_w", wy_words)
+        wb_w = load_fp8(nc.sync, "wb_w", wb_words[0])
+        for r in range(4):
+            load_scale_rows(nc.sync, wb_s, wb_scales, r)
+
+        ident = sb.tile([P, P], F32, name="ident")
+        make_identity(nc, ident[:])
+
+        zbank = [ps.tile([P, 512], F32, name="zbank%d" % c) for c in range(CHUNKS)]
+        obank = [ps.tile([P, 512], F32, name="obank%d" % c) for c in range(CHUNKS)]
+
+        def cols(c):
+            return slice(P * c, P * (c + 1))
+
+        first = [
+            (xt_w[0], xt_s[:, 0, :], wa_w[0][:, 0, :], wa_s[:, 0, :]),
+            (xt_w[1], xt_s[:, 1, :], wa_w[1][:, 0, :], wa_s[:, 1, :]),
+            (xq_w, xq_s[:, 0, :], wc_w[:, 0, :], wc_s[:, 0, :]),
+        ]
+        zt = []
+        for g, (xw, xs, ww, ws) in enumerate(first):
+            for c in range(CHUNKS):
+                nc.tensor.matmul_mx(
+                    out=zbank[c][:], lhsT=xw[:, cols(c)].bitcast(FP8X4), lhsT_scale=xs[:, cols(c)],
+                    rhs=ww.bitcast(FP4X4), rhs_scale=ws, start=(g == 0), stop=(g == 2),
+                )
+        for c in range(CHUNKS):
+            t = sb.tile([P, 512], BF16, name="zt%d" % c, align_bytes=64)
+            zt.append(t)
+            dst = t[:].rearrange("p (u m e) -> p u m e", u=2, e=2)
+            src = zbank[c][:].rearrange("p (m u e) -> p u m e", u=2, e=2)
+            if c % 2 == 0:
+                nc.scalar.copy(out=dst, in_=src)
+            else:
+                nc.vector.tensor_copy(out=dst, in_=src)
+
+        pieces = [(0, 0, 4, obank[0]), (1, 0, 4, obank[1]), (2, 0, 4, obank[2]), (3, 0, 2, obank[3]), (3, 2, 2, zbank[0])]
+
+        def skip(piece):
+            c, i0, ni, bank = piece
+            for z in range(2):
+                for i in range(ni):
+                    nc.tensor.matmul_mx(
+                        out=bank[:, cols(i)],
+                        lhsT=wy_w[:, z, 2 * P * (i0 + i) : 2 * P * (i0 + i + 1)].bitcast(FP4X4),
+                        lhsT_scale=wy_s[:, z, cols(i0 + i)],
+                        rhs=xt_w[z][:, cols(c)].bitcast(FP8X4), rhs_scale=xt_s[:, z, cols(c)],
+                        start=(z == 0 and i == 0), stop=False,
+                    )
+
+        codes = [sb.tile([P, P], U32, name="codes%d" % c, align_bytes=64) for c in range(CHUNKS)]
+        hscale = [sb.tile([P, P], U8, name="hscale%d" % c, align_bytes=64) for c in range(CHUNKS)]
+        hid = [sb.tile([P, 512], BF16, name="hid%d" % c, align_bytes=64) for c in range(CHUNKS)]
+
+        def second(piece, engine):
+            c, i0, ni, bank = piece
+            for i in range(ni):
+                nc.tensor.matmul_mx(
+                    out=bank[:, cols(i)],
+                    lhsT=wb_w[:, cols(i0 + i)].bitcast(FP8X4), lhsT_scale=wb_s[:, 0, cols(i0 + i)],
+                    rhs=codes[c][:].bitcast(FP8X4), rhs_scale=hscale[c][:],
+                    start=False, stop=(i == ni - 1),
+                )
+            res = sb.tile([P, ni * P], F32, name="res%d_%d" % (c, i0))
+            if engine == "scalar":
+                nc.scalar.copy(out=res[:], in_=bank[:, 0 : ni * P])
+            else:
+                nc.vector.tensor_copy(out=res[:], in_=bank[:, 0 : ni * P])
+            dst = out[P * i0 : P * (i0 + ni), cols(c)].rearrange("(i p) t -> p i t", p=P)
+            nc.sync.dma_start(out=dst, in_=res[:].rearrange("p (i t) -> p i t", t=P))
+
+        def peak(c):
+            lo = PAD + 512 * c
+            nc.vector.tensor_tensor(
+                out=hid[c][:], in0=zb[:, lo : lo + 512], in1=zb[:, lo - 4 : lo + 508], op=mybir.AluOpType.max
+            )
+
+        def quantize(c):
+            nc.vector.quantize_mx(out=codes[c][:].bitcast(FP8X4), scales=hscale[c][:], in_=hid[c][:])
+
+        skip(pieces[0])
+        for c in range(CHUNKS):
+            words = zt[c][:].bitcast(F32)
+            for u in range(2):
+                nc.tensor.transpose(zbank[c][:, cols(u)], words[:, cols(u)], ident[:])
+            lo = PAD + 512 * c
+            nc.scalar.copy(
+                out=zb[:, lo : lo + 512].bitcast(F32).rearrange("p (t u) -> p t u", u=2),
+                in_=zbank[c][:, 0 : 2 * P].rearrange("p (u t) -> p t u", u=2),
+            )
+        peak(0)
+        for c in range(1, CHUNKS):
+            peak(c)
+            quantize(c - 1)
+        quantize(CHUNKS - 1)
+
+        skip(pieces[1])
+        second(pieces[0], "scalar")
+        skip(pieces[2])
+        second(pieces[1], "vector")
+        second(pieces[2], "scalar")
+        skip(pieces[3])
+        second(pieces[3], "vector")
+        skip(pieces[4])
+        second(pieces[4], "scalar")

@@ -17,6 +17,7 @@ FP4X4 = mybir.dt.float4_e2m1fn_x4
 P = 128
 CHUNKS = T // P
 PAD = 32
+WARM = 20
 
 
 def tile_mix_hidden_peak_with_before_kernel(
@@ -50,12 +51,15 @@ def tile_mix_hidden_peak_with_before_kernel(
 
         xt_s = plane(nc.vector, "xt_s", xt_scales)
         wa_s = plane(nc.gpsimd, "wa_s", wa_scales)
+        zb = sb.tile([P, PAD + 4 * T], BF16, name="zb", align_bytes=64)
+        nc.vector.memset(zb[:, 0:512], 0.0)
         xq_s = plane(nc.vector, "xq_s", xq_scales)
+        codes = [sb.tile([P, P], U32, name="codes%d" % c, align_bytes=64) for c in range(CHUNKS)]
+        hscale = [sb.tile([P, P], U8, name="hscale%d" % c, align_bytes=64) for c in range(CHUNKS)]
+        nc.vector.quantize_mx(out=codes[3][:].bitcast(FP8X4), scales=hscale[3][:], in_=zb[:, 0:512])
         wy_s = plane(nc.vector, "wy_s", wy_scales)
         wc_s = plane(nc.vector, "wc_s", wc_scales)
         wb_s = plane(nc.vector, "wb_s", wb_scales)
-        zb = sb.tile([P, PAD + 4 * T], BF16, name="zb", align_bytes=64)
-        nc.vector.memset(zb[:, 0:PAD], 0.0)
 
         wa_w = [load_fp4(nc.scalar, "wa_w0", wa_words[0:1])]
         xt_w = [load_fp8(nc.scalar, "xt_w0", xt_words[0])]
@@ -87,6 +91,12 @@ def tile_mix_hidden_peak_with_before_kernel(
 
         def cols(c):
             return slice(P * c, P * (c + 1))
+
+        for w in range(WARM):
+            nc.tensor.matmul_mx(
+                out=obank[3][:, 0:P], lhsT=codes[3][:].bitcast(FP8X4), lhsT_scale=hscale[3][:],
+                rhs=codes[3][:].bitcast(FP8X4), rhs_scale=hscale[3][:], start=True, stop=True,
+            )
 
         first = [
             (xt_w[0], xt_s[:, 0, :], wa_w[0][:, 0, :], wa_s[:, 0, :]),
@@ -124,8 +134,6 @@ def tile_mix_hidden_peak_with_before_kernel(
                         start=(z == 0 and i == 0), stop=False,
                     )
 
-        codes = [sb.tile([P, P], U32, name="codes%d" % c, align_bytes=64) for c in range(CHUNKS)]
-        hscale = [sb.tile([P, P], U8, name="hscale%d" % c, align_bytes=64) for c in range(CHUNKS)]
         hid = [sb.tile([P, 512], BF16, name="hid%d" % c, align_bytes=64) for c in range(CHUNKS)]
 
         def second(piece, engine):

from contextlib import ExitStack

import concourse.mybir as mybir
from concourse.masks import make_identity

K, L, T, R, N = 1024, 512, 512, 512, 512
FLOPS = 2 * T * (K * R + L * R + R * N + K * N)

F32 = mybir.dt.float32
BF16 = mybir.dt.bfloat16
I32 = mybir.dt.int32
U32 = mybir.dt.uint32
U8 = mybir.dt.uint8
FP8X4 = mybir.dt.float8_e4m3fn_x4
FP4X4 = mybir.dt.float4_e2m1fn_x4

P = 128
CHUNKS = T // P
PAD = 32
WARM = 20


def tile_mix_hidden_peak_with_before_kernel(
    tc, xt_words, xt_scales, wa_words, wa_scales, xq_words, xq_scales,
    wc_words, wc_scales, wb_words, wb_scales, wy_words, wy_scales, out,
):
    nc = tc.nc
    with ExitStack() as ctx:
        sb = ctx.enter_context(tc.tile_pool(name="sb", bufs=1))
        ps = ctx.enter_context(tc.psum_pool(name="ps", bufs=1))
        ctx.enter_context(tc.manual_schedule())

        def plane(engine, name, scales):
            t = sb.tile([P, scales.shape[0], 512], U8, name=name, align_bytes=64)
            engine.memset(t[:].bitcast(I32), 0)
            return t

        def load_scale_rows(queue, t, scales, r):
            rows = scales.rearrange("z (q r) c -> r q z c", r=4)
            queue.dma_start(out=t[r:P:32, :, :].bitcast(I32), in_=rows[r].bitcast(I32))

        def load_fp8(queue, name, words):
            t = sb.tile([P, 512], U32, name=name, align_bytes=64)
            queue.dma_start(out=t[:].bitcast(I32), in_=words.rearrange("p n b -> p (n b)").bitcast(I32))
            return t

        def load_fp4(queue, name, words):
            t = sb.tile([P, words.shape[0], 1024], U8, name=name, align_bytes=64)
            queue.dma_start(out=t[:].bitcast(I32), in_=words.rearrange("z p b -> p z b").bitcast(I32))
            return t

        xt_s = plane(nc.vector, "xt_s", xt_scales)
        wa_s = plane(nc.gpsimd, "wa_s", wa_scales)
        zb = sb.tile([P, PAD + 4 * T], BF16, name="zb", align_bytes=64)
        nc.vector.memset(zb[:, 0:512], 0.0)
        xq_s = plane(nc.vector, "xq_s", xq_scales)
        codes = [sb.tile([P, P], U32, name="codes%d" % c, align_bytes=64) for c in range(CHUNKS)]
        hscale = [sb.tile([P, P], U8, name="hscale%d" % c, align_bytes=64) for c in range(CHUNKS)]
        nc.vector.quantize_mx(out=codes[3][:].bitcast(FP8X4), scales=hscale[3][:], in_=zb[:, 0:512])
        wy_s = plane(nc.vector, "wy_s", wy_scales)
        wc_s = plane(nc.vector, "wc_s", wc_scales)
        wb_s = plane(nc.vector, "wb_s", wb_scales)

        wa_w = [load_fp4(nc.scalar, "wa_w0", wa_words[0:1])]
        xt_w = [load_fp8(nc.scalar, "xt_w0", xt_words[0])]
        load_scale_rows(nc.gpsimd, wa_s, wa_scales, 3)
        for r in range(4):
            load_scale_rows(nc.sync, xt_s, xt_scales, r)
        for r in range(3):
            load_scale_rows(nc.sync, wa_s, wa_scales, r)
        for r in range(4):
            load_scale_rows(nc.gpsimd, wy_s, wy_scales, r)
        xt_w.append(load_fp8(nc.sync, "xt_w1", xt_words[1]))
        wa_w.append(load_fp4(nc.sync, "wa_w1", wa_words[1:2]))
        for r in range(4):
            load_scale_rows(nc.sync, xq_s, xq_scales, r)
        xq_w = load_fp8(nc.sync, "xq_w", xq_words[0])
        wc_w = load_fp4(nc.sync, "wc_w", wc_words)
        for r in range(4):
            load_scale_rows(nc.sync, wc_s, wc_scales, r)
        wy_w = load_fp4(nc.sync, "wy_w", wy_words)
        wb_w = load_fp8(nc.sync, "wb_w", wb_words[0])
        for r in range(4):
            load_scale_rows(nc.sync, wb_s, wb_scales, r)

        ident = sb.tile([P, P], F32, name="ident")
        make_identity(nc, ident[:])

        zbank = [ps.tile([P, 512], F32, name="zbank%d" % c) for c in range(CHUNKS)]
        obank = [ps.tile([P, 512], F32, name="obank%d" % c) for c in range(CHUNKS)]

        def cols(c):
            return slice(P * c, P * (c + 1))

        for w in range(WARM):
            nc.tensor.matmul_mx(
                out=obank[3][:, 0:P], lhsT=codes[3][:].bitcast(FP8X4), lhsT_scale=hscale[3][:],
                rhs=codes[3][:].bitcast(FP8X4), rhs_scale=hscale[3][:], start=True, stop=True,
            )

        first = [
            (xt_w[0], xt_s[:, 0, :], wa_w[0][:, 0, :], wa_s[:, 0, :]),
            (xt_w[1], xt_s[:, 1, :], wa_w[1][:, 0, :], wa_s[:, 1, :]),
            (xq_w, xq_s[:, 0, :], wc_w[:, 0, :], wc_s[:, 0, :]),
        ]
        zt = []
        for g, (xw, xs, ww, ws) in enumerate(first):
            for c in range(CHUNKS):
                nc.tensor.matmul_mx(
                    out=zbank[c][:], lhsT=xw[:, cols(c)].bitcast(FP8X4), lhsT_scale=xs[:, cols(c)],
                    rhs=ww.bitcast(FP4X4), rhs_scale=ws, start=(g == 0), stop=(g == 2),
                )
        for c in range(CHUNKS):
            t = sb.tile([P, 512], BF16, name="zt%d" % c, align_bytes=64)
            zt.append(t)
            dst = t[:].rearrange("p (u m e) -> p u m e", u=2, e=2)
            src = zbank[c][:].rearrange("p (m u e) -> p u m e", u=2, e=2)
            if c % 2 == 0:
                nc.scalar.copy(out=dst, in_=src)
            else:
                nc.vector.tensor_copy(out=dst, in_=src)

        pieces = [(0, 0, 4, obank[0]), (1, 0, 4, obank[1]), (2, 0, 4, obank[2]), (3, 0, 2, obank[3]), (3, 2, 2, zbank[0])]

        def skip(piece):
            c, i0, ni, bank = piece
            for z in range(2):
                for i in range(ni):
                    nc.tensor.matmul_mx(
                        out=bank[:, cols(i)],
                        lhsT=wy_w[:, z, 2 * P * (i0 + i) : 2 * P * (i0 + i + 1)].bitcast(FP4X4),
                        lhsT_scale=wy_s[:, z, cols(i0 + i)],
                        rhs=xt_w[z][:, cols(c)].bitcast(FP8X4), rhs_scale=xt_s[:, z, cols(c)],
                        start=(z == 0 and i == 0), stop=False,
                    )

        hid = [sb.tile([P, 512], BF16, name="hid%d" % c, align_bytes=64) for c in range(CHUNKS)]

        def second(piece, engine):
            c, i0, ni, bank = piece
            for i in range(ni):
                nc.tensor.matmul_mx(
                    out=bank[:, cols(i)],
                    lhsT=wb_w[:, cols(i0 + i)].bitcast(FP8X4), lhsT_scale=wb_s[:, 0, cols(i0 + i)],
                    rhs=codes[c][:].bitcast(FP8X4), rhs_scale=hscale[c][:],
                    start=False, stop=(i == ni - 1),
                )
            res = sb.tile([P, ni * P], F32, name="res%d_%d" % (c, i0))
            if engine == "scalar":
                nc.scalar.copy(out=res[:], in_=bank[:, 0 : ni * P])
            else:
                nc.vector.tensor_copy(out=res[:], in_=bank[:, 0 : ni * P])
            dst = out[P * i0 : P * (i0 + ni), cols(c)].rearrange("(i p) t -> p i t", p=P)
            nc.sync.dma_start(out=dst, in_=res[:].rearrange("p (i t) -> p i t", t=P))

        def peak(c):
            lo = PAD + 512 * c
            nc.vector.tensor_tensor(
                out=hid[c][:], in0=zb[:, lo : lo + 512], in1=zb[:, lo - 4 : lo + 508], op=mybir.AluOpType.max
            )

        def quantize(c):
            nc.vector.quantize_mx(out=codes[c][:].bitcast(FP8X4), scales=hscale[c][:], in_=hid[c][:])

        skip(pieces[0])
        for c in range(CHUNKS):
            words = zt[c][:].bitcast(F32)
            for u in range(2):
                nc.tensor.transpose(zbank[c][:, cols(u)], words[:, cols(u)], ident[:])
            lo = PAD + 512 * c
            nc.scalar.copy(
                out=zb[:, lo : lo + 512].bitcast(F32).rearrange("p (t u) -> p t u", u=2),
                in_=zbank[c][:, 0 : 2 * P].rearrange("p (u t) -> p t u", u=2),
            )
        peak(0)
        for c in range(1, CHUNKS):
            peak(c)
            quantize(c - 1)
        quantize(CHUNKS - 1)

        skip(pieces[1])
        second(pieces[0], "scalar")
        skip(pieces[2])
        second(pieces[1], "vector")
        second(pieces[2], "scalar")
        skip(pieces[3])
        second(pieces[3], "vector")
        skip(pieces[4])
        second(pieces[4], "scalar")
